import numpy as np
import ml_dtypes


def mxq(x, axis, fmt="e4m3"):
    dtype, down = {"e4m3": (ml_dtypes.float8_e4m3fn, 7), "e5m2": (ml_dtypes.float8_e5m2, 14)}[fmt]
    v = np.moveaxis(np.asarray(x, np.float32).astype(ml_dtypes.bfloat16).astype(np.float64), axis, -1)
    blocks = v.reshape(v.shape[:-1] + (-1, 32))
    amax = np.abs(blocks).max(-1, keepdims=True)
    byte = np.maximum(np.where(amax > 0, np.frexp(amax)[1] - 1 + 127, 0) - down, 1)
    scale = np.exp2(byte - 127.0)
    codes = (blocks / scale).astype(np.float32).astype(dtype).astype(np.float64)
    return np.moveaxis((codes * scale).reshape(v.shape), -1, axis)


WIDE = False


def mx_kscale(k):
    if not WIDE:
        return np.ones(k)
    levels = np.array([10, -10, 5, -5, 0])
    if k % 512:
        return np.exp2(np.random.permutation(np.resize(levels, k // 32))).repeat(32)
    a = np.empty((k // 512, 16))
    for p in range(k // 512):
        a[p, :8] = np.random.permutation(np.resize(levels, 8))
        for g in range(8):
            far = levels[np.abs(levels - a[p, g]) >= 10]
            a[p, g + 8] = far[np.random.randint(len(far))]
    return np.exp2(a.ravel()).repeat(32)


def f64(x):
    return np.asarray(x).astype(np.float64)


def striped(idx):
    return np.tile(idx.reshape(-1, 16).T, (8, 1)).astype(np.uint16)


def unstriped(offs):
    return offs[:16].T.reshape(-1).astype(np.int64)


E2M1 = np.array([0.0, 0.5, 1.0, 1.5, 2.0, 3.0, 4.0, 6.0, -0.0, -0.5, -1.0, -1.5, -2.0, -3.0, -4.0, -6.0])


def pack_weight(w, fmt):
    k, n = w.shape
    w = f64(np.asarray(w, np.float32).astype(ml_dtypes.bfloat16)).reshape(k // 32, 32, n)
    amax = np.abs(w).max(1)
    if fmt == "e4m3":
        byte = np.frexp(amax)[1] - 1 + 127 - 7
    else:
        mant, ex = np.frexp(amax / 6.0)
        byte = np.where(mant > 0.5, ex, ex - 1) + 127
    byte = np.clip(np.where(amax > 0, byte, 1), 1, 254)
    scaled = (w * np.exp2(127.0 - byte)[:, None, :]).reshape(k, n).astype(np.float32)
    by_word = np.ascontiguousarray(scaled.reshape(k // 512, 128, 4, n).transpose(0, 1, 3, 2))
    if fmt == "e4m3":
        words = by_word.astype(ml_dtypes.float8_e4m3fn).view(np.uint8)
    else:
        c = by_word.astype(ml_dtypes.float4_e2m1fn).view(np.uint8) & 0xF
        words = (c[..., 0::2] | (c[..., 1::2] << 4)).reshape(k // 512, 128, 2 * n)
    return np.ascontiguousarray(words), np.ascontiguousarray(byte.astype(np.uint8).reshape(k // 512, 16, n))


def unpack_weight(words, scales, fmt):
    g, _, n = scales.shape
    words = np.ascontiguousarray(words).reshape(g, 128, n, -1)
    if fmt == "e4m3":
        vals = words.view(ml_dtypes.float8_e4m3fn).astype(np.float64)
    else:
        nib = np.empty((g, 128, n, 4), np.uint8)
        nib[..., 0::2] = words & 0xF
        nib[..., 1::2] = words >> 4
        vals = E2M1[nib]
    vals = vals * np.repeat(np.exp2(scales.astype(np.float64) - 127.0), 8, axis=1)[..., None]
    return vals.transpose(0, 1, 3, 2).reshape(g * 512, n)


def gelu(v):
    return 0.5 * v * (1.0 + np.tanh(np.sqrt(2.0 / np.pi) * (v + 0.044715 * v**3)))


K, T, S, H, T2, P, N = 1536, 4096, 1024, 512, 2048, 1024, 768

def setup_inputs():
    n = np.random.standard_normal
    s = mx_kscale(K)[:, None]
    u = mx_kscale(H)[:, None]
    d = {}
    d["tab_words"], d["tab_scales"] = pack_weight(n((K, T)) * s, "e4m3")
    d["offs"] = striped(np.random.permutation(T)[:S])
    d["w1"] = (n((K, H)) / K**0.5 / s * u.T).astype(np.float32)
    d["cap"] = ((0.6 + 0.4 * n(H)) * u[:, 0]).astype(np.float32)
    d["page0"] = (n((H, T2)) * u).astype(np.float32)
    d["wgs"] = np.exp(0.3 * n((128, S))).astype(np.float32)
    d["offs2"] = striped(np.random.permutation(T2)[:S])
    d["offs3"] = striped(np.random.permutation(T2)[:P])
    d["low"] = ((-0.7 + 0.4 * n(H)) * u[:, 0]).astype(np.float32)
    d["w2_words"], d["w2_scales"] = pack_weight(2.4 * n((H, N)) / H**0.5 / u, "e2m1")
    d["w3"] = (n((H, N)) / H**0.5 / u).astype(np.float32)
    d["gain"] = np.exp(0.3 * n(N)).astype(np.float32)
    d["page1"] = n((N, T2)).astype(np.float32)
    d["wgo"] = np.exp(0.3 * n((128, P))).astype(np.float32)
    d["offs4"] = striped(np.random.permutation(T2)[:P])
    return d

def reference(tab_words, tab_scales, offs, w1, cap, page0, wgs, offs2, offs3, low, w2_words, w2_scales, w3, gain, page1, wgo, offs4):
    v = unpack_weight(tab_words, tab_scales, "e4m3")[:, unstriped(offs)]
    h = mxq(f64(w1), 0, "e4m3").T @ v
    h = np.minimum(h, f64(cap)[:, None])
    page = f64(page0).copy()
    page[:, unstriped(offs2)] = np.tile(f64(wgs), (H // 128, 1)) * h
    x = page[:, unstriped(offs3)]
    x = np.maximum(x, f64(low)[:, None])
    w2 = unpack_weight(w2_words, w2_scales, "e2m1")
    b = w2.T @ mxq(x, 0, "e4m3")
    e = mxq(f64(w3), 0, "e4m3").T @ mxq(h, 0, "e4m3")
    y = b / (1.0 + np.exp(-b)) - f64(gain)[:, None] * e
    out = f64(page1).copy()
    out[:, unstriped(offs4)] = np.tile(f64(wgo), (N // 128, 1)) * y
    return out

@@ -1,0 +1,312 @@
+from contextlib import ExitStack
+
+import concourse.mybir as mybir
+from concourse.masks import make_identity
+
+K, T, S, H, T2, N = 1536, 4096, 1024, 512, 2048, 768
+FLOPS = 2 * S * (K * H + 2 * H * N)
+
+F32 = mybir.dt.float32
+BF16 = mybir.dt.bfloat16
+I32 = mybir.dt.int32
+U32 = mybir.dt.uint32
+U16 = mybir.dt.uint16
+U8 = mybir.dt.uint8
+FP8X4 = mybir.dt.float8_e4m3fn_x4
+FP4X4 = mybir.dt.float4_e2m1fn_x4
+ALU = mybir.AluOpType
+ACT = mybir.ActivationFunctionType
+
+P = 128
+PACK = 4
+PASSES = K // (P * PACK)
+HALF = 512
+HALVES = S // HALF
+N_TILES = N // P
+KIB = 1024
+X_SLICES = ((0, 256), (256, 256), (512, 512))
+EARLY_GE = 10
+
+
+def tile_list_binding_setting_page_kernel(
+    tc, tab_words, tab_scales, offs, w1, cap, page0, wgs, offs2, offs3, low, w2_words, w2_scales, w3, gain, page1, wgo, offs4, out
+):
+    nc = tc.nc
+
+    with ExitStack() as ctx:
+        lists = ctx.enter_context(tc.tile_pool(name="lists", bufs=1))
+        keep = ctx.enter_context(tc.tile_pool(name="keep", bufs=1))
+        ring = ctx.enter_context(tc.tile_pool(name="ring", bufs=2))
+        laid = ctx.enter_context(tc.tile_pool(name="laid", bufs=1))
+        psum = ctx.enter_context(tc.psum_pool(name="psum", bufs=8))
+
+        def placed(name, shape, dtype, kib):
+            return laid.tile(shape, dtype, name=name, offset=kib * KIB, align_bytes=64)
+
+        def kept(name, shape, dtype):
+            return keep.tile(shape, dtype, name=name, align_bytes=64)
+
+        def entries(offsets, first, count):
+            return offsets[:, first // 16 : (first + count) // 16]
+
+        def interleave(engine_copy, dst, src):
+            engine_copy(
+                out=dst.rearrange("p (c i) t -> p c t i", i=PACK),
+                in_=src.rearrange("p t (c i) -> p c t i", i=PACK),
+            )
+
+        def quantise(codes, scales, grouped):
+            nc.vector.quantize_mx(out=codes.bitcast(FP8X4), scales=scales, in_=grouped.rearrange("p c t -> p (c t)"))
+
+        idx = lists.tile([P, S // 16], U16, name="idx")
+        idx2 = lists.tile([P, S // 16], U16, name="idx2")
+        idx3 = lists.tile([P, S // 16], U16, name="idx3")
+        idx4 = lists.tile([P, S // 16], U16, name="idx4")
+
+        tab_plane = kept("tab_plane", [P, T], U8)
+        nc.gpsimd.memset(tab_plane[:].bitcast(I32), 0)
+        for q in range(4):
+            nc.gpsimd.dma_start(
+                out=tab_plane[32 * q : 32 * q + 4 * PASSES, :].bitcast(I32),
+                in_=tab_scales[:, 4 * q : 4 * q + 4, :].bitcast(I32),
+            )
+        w2_plane = kept("w2_plane", [P, N], U8)
+        nc.gpsimd.memset(w2_plane[:].bitcast(I32), 0)
+        for q in range(4):
+            nc.gpsimd.dma_start(
+                out=w2_plane[32 * q : 32 * q + 4, :].bitcast(I32),
+                in_=w2_scales[0, 4 * q : 4 * q + 4, :].bitcast(I32),
+            )
+        ident = kept("ident", [P, P], F32)
+        make_identity(nc, ident[:])
+
+        cap_sb = kept("cap_sb", [P, PACK], F32)
+        low_sb = kept("low_sb", [P, PACK], F32)
+        gain_sb = kept("gain_sb", [P, N_TILES], F32)
+        nc.scalar.dma_start(out=cap_sb[:], in_=cap.rearrange("(p t) -> p t", t=PACK))
+        nc.scalar.dma_start(out=low_sb[:], in_=low.rearrange("(p t) -> p t", t=PACK))
+        with nc.allow_non_contiguous_dma(reason="one gain value a partition and output tile"):
+            nc.scalar.dma_start(out=gain_sb[:], in_=gain.rearrange("(c p) -> p c", p=P))
+
+        tab = [placed(f"tab{a}", [P, T], I32, 16 * a) for a in range(PASSES)]
+        w1_raw = [placed(f"w1_raw{a}", [P, PACK, H], F32, 48 + 8 * a) for a in range(PASSES)]
+        states = [placed(f"states{t}", [P, T2], F32, 72 + 8 * t) for t in range(PACK)]
+        wgs_first = placed("wgs_first", [P, S], F32, 104)
+        wgs_rest = placed("wgs_rest", [P, PACK - 1, S], F32, 108)
+        w3_raw = placed("w3_raw", [P, PACK, N], F32, 136)
+        w2_codes = kept("w2_codes", [P, 2 * N], U8)
+        wgo_sb = kept("wgo_sb", [P, S], F32)
+
+        def load_tab(a):
+            nc.sync.dma_start(out=tab[a][:], in_=tab_words[a].rearrange("p t i -> p (t i)").bitcast(I32))
+
+        page0_rows = page0.rearrange("(p t) c -> t p c", t=PACK)
+        wgs_rows = wgs.rearrange("(q t) s -> q t s", t=PACK)
+
+        nc.sync.dma_start(idx[:], offs)
+        load_tab(0)
+        for a in range(PASSES):
+            nc.sync.dma_start(out=w1_raw[a][:], in_=w1[512 * a : 512 * (a + 1), :].rearrange("(p j) r -> p j r", j=PACK))
+        load_tab(1)
+        load_tab(2)
+        nc.sync.dma_start(idx2[:], offs2)
+        nc.sync.dma_start(out=states[0][:], in_=page0_rows[0])
+        for q in range(4):
+            nc.sync.dma_start(out=wgs_first[32 * q : 32 * (q + 1), :], in_=wgs_rows[:, 0, :])
+        nc.sync.dma_start(out=states[1][:], in_=page0_rows[1])
+        for q in range(4):
+            nc.sync.dma_start(out=wgs_rest[32 * q : 32 * (q + 1), :, :], in_=wgs_rows[:, 1:, :])
+        nc.sync.dma_start(out=states[2][:], in_=page0_rows[2])
+        nc.sync.dma_start(out=w3_raw[:], in_=w3.rearrange("(p j) n -> p j n", j=PACK))
+        nc.sync.dma_start(out=states[3][:], in_=page0_rows[3])
+        nc.sync.dma_start(idx3[:], offs3)
+        nc.sync.dma_start(idx4[:], offs4)
+        nc.sync.dma_start(out=w2_codes[:].bitcast(I32), in_=w2_words[0].bitcast(I32))
+        nc.sync.dma_start(out=wgo_sb[:], in_=wgo)
+
+        neg_gain = kept("neg_gain", [P, N_TILES], F32)
+        nc.gpsimd.tensor_scalar(out=neg_gain[:], in0=gain_sb[:], scalar1=-1.0, scalar2=0.0, op0=ALU.mult, op1=ALU.add)
+
+        picked = [kept(f"picked{a}", [P, S], U32) for a in range(PASSES)]
+        picked_plane = kept("picked_plane", [P, S], U8)
+        w1_codes = [kept(f"w1_codes{a}", [P, H], U32) for a in range(PASSES)]
+        w1_scales = [kept(f"w1_scales{a}", [P, H], U8) for a in range(PASSES)]
+
+        def pick_words(a, first, count):
+            nc.vector.tensor_copy(
+                out=picked[a][:, first : first + count],
+                in_=tab[a][:].bitcast(U32).indirect(entries(idx, first, count)),
+            )
+
+        def quantise_w1(a, engine_copy):
+            grouped = placed(f"w1_grouped{a}", [P, H, PACK], BF16, 160 + 4 * a)
+            engine_copy(
+                out=grouped[:].rearrange("p (t m) j -> p m t j", t=PACK),
+                in_=w1_raw[a][:].rearrange("p j (m t) -> p m t j", t=PACK),
+            )
+            quantise(w1_codes[a][:], w1_scales[a][:], grouped[:])
+
+        h_banks = {}
+
+        def first_product(a, u):
+            cols = slice(u * HALF, (u + 1) * HALF)
+            for t in range(PACK):
+                if a == 0:
+                    h_banks[t, u] = psum.tile([P, HALF], F32, name="bank")
+                rows = slice(t * P, (t + 1) * P)
+                nc.tensor.matmul_mx(
+                    out=h_banks[t, u][:],
+                    lhsT=w1_codes[a][:, rows].bitcast(FP8X4),
+                    lhsT_scale=w1_scales[a][:, rows],
+                    rhs=picked[a][:, cols].bitcast(FP8X4),
+                    rhs_scale=picked_plane[4 * a :, cols],
+                    start=(a == 0),
+                    stop=(a == PASSES - 1),
+                )
+
+        pick_words(0, 0, S)
+        nc.vector.tensor_copy(out=picked_plane[:], in_=tab_plane[:].indirect(idx[:]))
+        quantise_w1(0, nc.scalar.copy)
+        quantise_w1(1, nc.vector.tensor_copy)
+        quantise_w1(2, nc.scalar.copy)
+        pick_words(1, 0, S)
+        for a in range(PASSES - 1):
+            for u in range(HALVES):
+                first_product(a, u)
+        for u in range(HALVES):
+            pick_words(PASSES - 1, u * HALF, HALF)
+            first_product(PASSES - 1, u)
+
+        settings = [placed(f"settings{c}", [P, T2], F32, 8 * c) for c in range(N_TILES)]
+        for c in range(N_TILES):
+            nc.sync.dma_start(out=settings[c][:], in_=page1[c * P : (c + 1) * P, :])
+
+        h = placed("h", [P, PACK, S], F32, 120)
+
+        def cap_h(t, u):
+            part = h[:, t, u * HALF : (u + 1) * HALF]
+            nc.scalar.copy(out=part, in_=h_banks[t, u][:])
+            nc.vector.tensor_scalar(out=part, in0=part, scalar1=cap_sb[:, t : t + 1], scalar2=None, op0=ALU.min)
+
+        def put_states(t, first, count):
+            cols = slice(first, first + count)
+            factors = wgs_first[:, cols] if t == 0 else wgs_rest[:, t - 1, cols]
+            nc.vector.tensor_tensor(states[t][:].indirect(entries(idx2, first, count)), h[:, t, cols], factors, ALU.mult)
+
+        cap_h(0, 0)
+        put_states(0, 0, HALF)
+        for u in range(HALVES):
+            for t in range(PACK):
+                if (t, u) != (0, 0):
+                    cap_h(t, u)
+        put_states(0, HALF, HALF)
+
+        h_codes = kept("h_codes", [P, S], U32)
+        h_scales = kept("h_scales", [P, S], U8)
+
+        def quantise_h(u):
+            cols = slice(u * HALF, (u + 1) * HALF)
+            grouped = placed(f"h_grouped{u}", [P, HALF, PACK], BF16, 152 + 4 * u)
+            interleave(nc.scalar.copy, grouped[:], h[:, :, cols])
+            quantise(h_codes[:, cols], h_scales[:, cols], grouped[:])
+
+        w3_codes = kept("w3_codes", [P, N], U32)
+        w3_scales = kept("w3_scales", [P, N], U8)
+        put_states(1, 0, S)
+        quantise_h(0)
+        w3_grouped = placed("w3_grouped", [P, N, PACK], BF16, 160)
+        interleave(nc.scalar.copy, w3_grouped[:], w3_raw[:])
+        for first, count in ((0, 512), (512, 256)):
+            cols = slice(first, first + count)
+            quantise(w3_codes[:, cols], w3_scales[:, cols], w3_grouped[:, cols, :])
+        put_states(2, 0, S)
+        quantise_h(1)
+        put_states(3, 0, S)
+
+        fresh = {}
+
+        def fresh_term(u, c):
+            cols = slice(u * HALF, (u + 1) * HALF)
+            rows = slice(c * P, (c + 1) * P)
+            e_bank = psum.tile([P, HALF], F32, name="bank")
+            nc.tensor.matmul_mx(
+                out=e_bank[:],
+                lhsT=w3_codes[:, rows].bitcast(FP8X4),
+                lhsT_scale=w3_scales[:, rows],
+                rhs=h_codes[:, cols].bitcast(FP8X4),
+                rhs_scale=h_scales[:, cols],
+                start=True,
+                stop=True,
+            )
+            scaled = ring.tile([P, HALF], F32, name="scaled")
+            nc.scalar.activation(out=scaled[:], in_=e_bank[:], func=ACT.Copy, scale=neg_gain[:, c : c + 1])
+            turned_bank = psum.tile([P, HALF], F32, name="bank")
+            for b in range(HALF // P):
+                block = slice(b * P, (b + 1) * P)
+                nc.tensor.transpose(turned_bank[:, block], scaled[:, block], ident[:])
+            fresh[u, c] = placed(f"fresh{u}_{c}", [P, HALF], F32, 48 + 2 * (u * N_TILES + c))
+            nc.scalar.copy(out=fresh[u, c][:], in_=turned_bank[:])
+
+        fresh_order = [(u, c) for u in range(HALVES) for c in range(N_TILES)]
+        for u, c in fresh_order[:EARLY_GE]:
+            fresh_term(u, c)
+
+        x_codes = kept("x_codes", [P, S], U32)
+        x_scales = kept("x_scales", [P, S], U8)
+        fetched_at = (136, 140, 144)
+        grouped_at = (150, 152, 156)
+
+        def recall(s):
+            first, count = X_SLICES[s]
+            cols = slice(first, first + count)
+            x = placed(f"x{s}", [P, PACK, count], F32, fetched_at[s])
+            for t in range(PACK):
+                nc.vector.tensor_copy(out=x[:, t, :], in_=states[t][:].indirect(entries(idx3, first, count)))
+            for t in range(PACK):
+                nc.vector.tensor_scalar(out=x[:, t, :], in0=x[:, t, :], scalar1=low_sb[:, t : t + 1], scalar2=None, op0=ALU.max)
+            grouped = placed(f"x_grouped{s}", [P, count, PACK], BF16, grouped_at[s])
+            interleave(nc.scalar.copy, grouped[:], x[:])
+            quantise(x_codes[:, cols], x_scales[:, cols], grouped[:])
+
+        def settle(s, c):
+            first, count = X_SLICES[s]
+            blocks = count // P
+            b_bank = psum.tile([P, count], F32, name="bank")
+            for b in range(blocks):
+                cols = slice(first + b * P, first + (b + 1) * P)
+                nc.tensor.matmul_mx(
+                    out=b_bank[:, b * P : (b + 1) * P],
+                    lhsT=x_codes[:, cols].bitcast(FP8X4),
+                    lhsT_scale=x_scales[:, cols],
+                    rhs=w2_codes[:, 2 * c * P : 2 * (c + 1) * P].bitcast(FP4X4),
+                    rhs_scale=w2_plane[:, c * P : (c + 1) * P],
+                    start=True,
+                    stop=True,
+                )
+            gated = ring.tile([P, count], F32, name="gated")
+            nc.scalar.activation(out=gated[:], in_=b_bank[:], func=ACT.Silu)
+            y_bank = psum.tile([P, count], F32, name="bank")
+            u, within = divmod(first, HALF)
+            for b in range(blocks):
+                block = slice(b * P, (b + 1) * P)
+                term = fresh[u, c][:, within + b * P : within + (b + 1) * P]
+                nc.tensor.matmul(y_bank[:, block], lhsT=term, rhs=ident[:], start=True, stop=False, is_transpose=True)
+                nc.tensor.matmul(y_bank[:, block], lhsT=gated[:, block], rhs=ident[:], start=False, stop=True, is_transpose=True)
+            y = placed(f"y{s}_{c}", [P, count], F32, 104 + (first * N_TILES + c * count) * 4 // KIB)
+            nc.scalar.copy(out=y[:], in_=y_bank[:])
+            nc.vector.tensor_tensor(
+                settings[c][:].indirect(entries(idx4, first, count)), y[:], wgo_sb[:, first : first + count], ALU.mult
+            )
+
+        recall(0)
+        recall(1)
+        recall(2)
+        for c in range(N_TILES):
+            settle(0, c)
+        for u, c in fresh_order[EARLY_GE:]:
+            fresh_term(u, c)
+        for s in range(1, len(X_SLICES)):
+            for c in range(N_TILES):
+                settle(s, c)
+                if s == len(X_SLICES) - 1:
+                    nc.sync.dma_start(out=out[c * P : (c + 1) * P, :], in_=settings[c][:])

@@ -25,7 +25,7 @@ HALVES = S // HALF
 N_TILES = N // P
 KIB = 1024
 X_SLICES = ((0, 256), (256, 256), (512, 512))
-EARLY_GE = 10
+EARLY_GE = 12
 
 
 def tile_list_binding_setting_page_kernel(
@@ -64,19 +64,9 @@ def tile_list_binding_setting_page_kernel(
         idx4 = lists.tile([P, S // 16], U16, name="idx4")
 
         tab_plane = kept("tab_plane", [P, T], U8)
-        nc.gpsimd.memset(tab_plane[:].bitcast(I32), 0)
-        for q in range(4):
-            nc.gpsimd.dma_start(
-                out=tab_plane[32 * q : 32 * q + 4 * PASSES, :].bitcast(I32),
-                in_=tab_scales[:, 4 * q : 4 * q + 4, :].bitcast(I32),
-            )
+        nc.vector.memset(tab_plane[:].bitcast(I32), 0)
         w2_plane = kept("w2_plane", [P, N], U8)
-        nc.gpsimd.memset(w2_plane[:].bitcast(I32), 0)
-        for q in range(4):
-            nc.gpsimd.dma_start(
-                out=w2_plane[32 * q : 32 * q + 4, :].bitcast(I32),
-                in_=w2_scales[0, 4 * q : 4 * q + 4, :].bitcast(I32),
-            )
+        nc.vector.memset(w2_plane[:].bitcast(I32), 0)
         ident = kept("ident", [P, P], F32)
         make_identity(nc, ident[:])
 
@@ -84,15 +74,12 @@ def tile_list_binding_setting_page_kernel(
         low_sb = kept("low_sb", [P, PACK], F32)
         gain_sb = kept("gain_sb", [P, N_TILES], F32)
         nc.scalar.dma_start(out=cap_sb[:], in_=cap.rearrange("(p t) -> p t", t=PACK))
-        nc.scalar.dma_start(out=low_sb[:], in_=low.rearrange("(p t) -> p t", t=PACK))
-        with nc.allow_non_contiguous_dma(reason="one gain value a partition and output tile"):
-            nc.scalar.dma_start(out=gain_sb[:], in_=gain.rearrange("(c p) -> p c", p=P))
 
         tab = [placed(f"tab{a}", [P, T], I32, 16 * a) for a in range(PASSES)]
         w1_raw = [placed(f"w1_raw{a}", [P, PACK, H], F32, 48 + 8 * a) for a in range(PASSES)]
         states = [placed(f"states{t}", [P, T2], F32, 72 + 8 * t) for t in range(PACK)]
-        wgs_first = placed("wgs_first", [P, S], F32, 104)
-        wgs_rest = placed("wgs_rest", [P, PACK - 1, S], F32, 108)
+        wgs_sb = [placed(f"wgs{t}", [P, S], F32, kib) for t, kib in enumerate((104, 108, 136, 116))]
+        settings = [placed(f"settings{c}", [P, T2], F32, 8 * c) for c in range(N_TILES)]
         w3_raw = placed("w3_raw", [P, PACK, N], F32, 136)
         w2_codes = kept("w2_codes", [P, 2 * N], U8)
         wgo_sb = kept("wgo_sb", [P, S], F32)
@@ -105,27 +92,26 @@ def tile_list_binding_setting_page_kernel(
 
         nc.sync.dma_start(idx[:], offs)
         load_tab(0)
+        for q in range(4):
+            nc.sync.dma_start(
+                out=tab_plane[32 * q : 32 * q + 4 * PASSES, :].bitcast(I32),
+                in_=tab_scales[:, 4 * q : 4 * q + 4, :].bitcast(I32),
+            )
         for a in range(PASSES):
             nc.sync.dma_start(out=w1_raw[a][:], in_=w1[512 * a : 512 * (a + 1), :].rearrange("(p j) r -> p j r", j=PACK))
         load_tab(1)
         load_tab(2)
-        nc.sync.dma_start(idx2[:], offs2)
-        nc.sync.dma_start(out=states[0][:], in_=page0_rows[0])
-        for q in range(4):
-            nc.sync.dma_start(out=wgs_first[32 * q : 32 * (q + 1), :], in_=wgs_rows[:, 0, :])
-        nc.sync.dma_start(out=states[1][:], in_=page0_rows[1])
-        for q in range(4):
-            nc.sync.dma_start(out=wgs_rest[32 * q : 32 * (q + 1), :, :], in_=wgs_rows[:, 1:, :])
-        nc.sync.dma_start(out=states[2][:], in_=page0_rows[2])
-        nc.sync.dma_start(out=w3_raw[:], in_=w3.rearrange("(p j) n -> p j n", j=PACK))
-        nc.sync.dma_start(out=states[3][:], in_=page0_rows[3])
-        nc.sync.dma_start(idx3[:], offs3)
-        nc.sync.dma_start(idx4[:], offs4)
-        nc.sync.dma_start(out=w2_codes[:].bitcast(I32), in_=w2_words[0].bitcast(I32))
-        nc.sync.dma_start(out=wgo_sb[:], in_=wgo)
 
-        neg_gain = kept("neg_gain", [P, N_TILES], F32)
-        nc.gpsimd.tensor_scalar(out=neg_gain[:], in0=gain_sb[:], scalar1=-1.0, scalar2=0.0, op0=ALU.mult, op1=ALU.add)
+        def load_states(t):
+            nc.sync.dma_start(out=states[t][:], in_=page0_rows[t])
+
+        def load_wgs(t, first=0, count=S):
+            cols = slice(first, first + count)
+            for q in range(4):
+                nc.sync.dma_start(out=wgs_sb[t][32 * q : 32 * (q + 1), cols], in_=wgs_rows[:, t, cols])
+
+        def load_settings(c):
+            nc.sync.dma_start(out=settings[c][:], in_=page1[c * P : (c + 1) * P, :])
 
         picked = [kept(f"picked{a}", [P, S], U32) for a in range(PASSES)]
         picked_plane = kept("picked_plane", [P, S], U8)
@@ -169,17 +155,44 @@ def tile_list_binding_setting_page_kernel(
         quantise_w1(0, nc.scalar.copy)
         quantise_w1(1, nc.vector.tensor_copy)
         quantise_w1(2, nc.scalar.copy)
-        pick_words(1, 0, S)
-        for a in range(PASSES - 1):
-            for u in range(HALVES):
-                first_product(a, u)
         for u in range(HALVES):
-            pick_words(PASSES - 1, u * HALF, HALF)
-            first_product(PASSES - 1, u)
+            first_product(0, u)
+        for a in range(1, PASSES):
+            for u in range(HALVES):
+                pick_words(a, u * HALF, HALF)
+                first_product(a, u)
 
-        settings = [placed(f"settings{c}", [P, T2], F32, 8 * c) for c in range(N_TILES)]
-        for c in range(N_TILES):
-            nc.sync.dma_start(out=settings[c][:], in_=page1[c * P : (c + 1) * P, :])
+        nc.sync.dma_start(idx2[:], offs2)
+        load_states(0)
+        load_wgs(0, 0, HALF)
+        load_wgs(0, HALF, HALF)
+        nc.sync.dma_start(out=w3_raw[:], in_=w3.rearrange("(p j) n -> p j n", j=PACK))
+        load_states(1)
+        load_wgs(1)
+        with nc.allow_non_contiguous_dma(reason="one gain value a partition and output tile"):
+            nc.sync.dma_start(out=gain_sb[:], in_=gain.rearrange("(c p) -> p c", p=P))
+        load_states(2)
+        load_wgs(3)
+        load_settings(0)
+        load_settings(1)
+        load_settings(2)
+        load_states(3)
+        nc.sync.dma_start(idx3[:], offs3)
+        nc.sync.dma_start(idx4[:], offs4)
+        nc.sync.dma_start(out=low_sb[:], in_=low.rearrange("(p t) -> p t", t=PACK))
+        nc.sync.dma_start(out=w2_codes[:].bitcast(I32), in_=w2_words[0].bitcast(I32))
+        for q in range(4):
+            nc.sync.dma_start(
+                out=w2_plane[32 * q : 32 * q + 4, :].bitcast(I32),
+                in_=w2_scales[0, 4 * q : 4 * q + 4, :].bitcast(I32),
+            )
+        nc.sync.dma_start(out=wgo_sb[:], in_=wgo)
+        load_settings(3)
+        load_settings(4)
+        load_settings(5)
+
+        neg_gain = kept("neg_gain", [P, N_TILES], F32)
+        nc.gpsimd.tensor_scalar(out=neg_gain[:], in0=gain_sb[:], scalar1=-1.0, scalar2=0.0, op0=ALU.mult, op1=ALU.add)
 
         h = placed("h", [P, PACK, S], F32, 120)
 
@@ -190,7 +203,7 @@ def tile_list_binding_setting_page_kernel(
 
         def put_states(t, first, count):
             cols = slice(first, first + count)
-            factors = wgs_first[:, cols] if t == 0 else wgs_rest[:, t - 1, cols]
+            factors = wgs_sb[t][:, cols]
             nc.vector.tensor_tensor(states[t][:].indirect(entries(idx2, first, count)), h[:, t, cols], factors, ALU.mult)
 
         cap_h(0, 0)
@@ -216,11 +229,12 @@ def tile_list_binding_setting_page_kernel(
         quantise_h(0)
         w3_grouped = placed("w3_grouped", [P, N, PACK], BF16, 160)
         interleave(nc.scalar.copy, w3_grouped[:], w3_raw[:])
+        load_wgs(2)
         for first, count in ((0, 512), (512, 256)):
             cols = slice(first, first + count)
             quantise(w3_codes[:, cols], w3_scales[:, cols], w3_grouped[:, cols, :])
-        put_states(2, 0, S)
         quantise_h(1)
+        put_states(2, 0, S)
         put_states(3, 0, S)
 
         fresh = {}
@@ -238,7 +252,7 @@ def tile_list_binding_setting_page_kernel(
                 start=True,
                 stop=True,
             )
-            scaled = ring.tile([P, HALF], F32, name="scaled")
+            scaled = placed(f"scaled{u}_{c}", [P, HALF], F32, 150 + 2 * (c % 2))
             nc.scalar.activation(out=scaled[:], in_=e_bank[:], func=ACT.Copy, scale=neg_gain[:, c : c + 1])
             turned_bank = psum.tile([P, HALF], F32, name="bank")
             for b in range(HALF // P):
@@ -255,17 +269,22 @@ def tile_list_binding_setting_page_kernel(
         x_scales = kept("x_scales", [P, S], U8)
         fetched_at = (136, 140, 144)
         grouped_at = (150, 152, 156)
+        fetched = {}
 
         def recall(s):
             first, count = X_SLICES[s]
-            cols = slice(first, first + count)
             x = placed(f"x{s}", [P, PACK, count], F32, fetched_at[s])
             for t in range(PACK):
                 nc.vector.tensor_copy(out=x[:, t, :], in_=states[t][:].indirect(entries(idx3, first, count)))
             for t in range(PACK):
                 nc.vector.tensor_scalar(out=x[:, t, :], in0=x[:, t, :], scalar1=low_sb[:, t : t + 1], scalar2=None, op0=ALU.max)
+            fetched[s] = x
+
+        def quantise_x(s):
+            first, count = X_SLICES[s]
+            cols = slice(first, first + count)
             grouped = placed(f"x_grouped{s}", [P, count, PACK], BF16, grouped_at[s])
-            interleave(nc.scalar.copy, grouped[:], x[:])
+            interleave(nc.scalar.copy, grouped[:], fetched[s][:])
             quantise(x_codes[:, cols], x_scales[:, cols], grouped[:])
 
         def settle(s, c):
@@ -300,9 +319,12 @@ def tile_list_binding_setting_page_kernel(
 
         recall(0)
         recall(1)
+        quantise_x(0)
+        quantise_x(1)
         recall(2)
         for c in range(N_TILES):
             settle(0, c)
+        quantise_x(2)
         for u, c in fresh_order[EARLY_GE:]:
             fresh_term(u, c)
         for s in range(1, len(X_SLICES)):

@@ -25,7 +25,8 @@ HALVES = S // HALF
 N_TILES = N // P
 KIB = 1024
 X_SLICES = ((0, 256), (256, 256), (512, 512))
-EARLY_GE = 12
+W3_PARTS = ((0, 512), (512, 256))
+EARLY_GE = 9
 
 
 def tile_list_binding_setting_page_kernel(
@@ -63,8 +64,13 @@ def tile_list_binding_setting_page_kernel(
         idx3 = lists.tile([P, S // 16], U16, name="idx3")
         idx4 = lists.tile([P, S // 16], U16, name="idx4")
 
-        tab_plane = kept("tab_plane", [P, T], U8)
-        nc.vector.memset(tab_plane[:].bitcast(I32), 0)
+        tab_plane = placed("tab_plane", [P, T], U8, 180)
+        nc.gpsimd.memset(tab_plane[:].bitcast(I32), 0)
+        for q in range(4):
+            nc.gpsimd.dma_start(
+                out=tab_plane[32 * q : 32 * q + 4 * PASSES, :].bitcast(I32),
+                in_=tab_scales[:, 4 * q : 4 * q + 4, :].bitcast(I32),
+            )
         w2_plane = kept("w2_plane", [P, N], U8)
         nc.vector.memset(w2_plane[:].bitcast(I32), 0)
         ident = kept("ident", [P, P], F32)
@@ -77,26 +83,23 @@ def tile_list_binding_setting_page_kernel(
 
         tab = [placed(f"tab{a}", [P, T], I32, 16 * a) for a in range(PASSES)]
         w1_raw = [placed(f"w1_raw{a}", [P, PACK, H], F32, 48 + 8 * a) for a in range(PASSES)]
-        states = [placed(f"states{t}", [P, T2], F32, 72 + 8 * t) for t in range(PACK)]
-        wgs_sb = [placed(f"wgs{t}", [P, S], F32, kib) for t, kib in enumerate((104, 108, 136, 116))]
+        states = [placed(f"states{t}", [P, T2], F32, kib) for t, kib in enumerate((72, 80, 184, 176))]
+        wgs_pair = placed("wgs_pair", [P, 2 * S], F32, 104)
+        wgs_late = [placed(f"wgs{t}", [P, S], F32, kib) for t, kib in ((2, 172), (3, 192))]
+        wgs_sb = [wgs_pair[:, :S], wgs_pair[:, S:], wgs_late[0][:], wgs_late[1][:]]
         settings = [placed(f"settings{c}", [P, T2], F32, 8 * c) for c in range(N_TILES)]
-        w3_raw = placed("w3_raw", [P, PACK, N], F32, 136)
+        w3_raw = [placed(f"w3_raw{i}", [P, PACK, count], F32, (172, 192)[i]) for i, (first, count) in enumerate(W3_PARTS)]
         w2_codes = kept("w2_codes", [P, 2 * N], U8)
-        wgo_sb = kept("wgo_sb", [P, S], F32)
+        wgo_sb = placed("wgo_sb", [P, S], F32, 88)
 
         def load_tab(a):
             nc.sync.dma_start(out=tab[a][:], in_=tab_words[a].rearrange("p t i -> p (t i)").bitcast(I32))
 
         page0_rows = page0.rearrange("(p t) c -> t p c", t=PACK)
-        wgs_rows = wgs.rearrange("(q t) s -> q t s", t=PACK)
+        wgs_rows = wgs.rearrange("(q t) s -> q (t s)", t=PACK)
 
         nc.sync.dma_start(idx[:], offs)
         load_tab(0)
-        for q in range(4):
-            nc.sync.dma_start(
-                out=tab_plane[32 * q : 32 * q + 4 * PASSES, :].bitcast(I32),
-                in_=tab_scales[:, 4 * q : 4 * q + 4, :].bitcast(I32),
-            )
         for a in range(PASSES):
             nc.sync.dma_start(out=w1_raw[a][:], in_=w1[512 * a : 512 * (a + 1), :].rearrange("(p j) r -> p j r", j=PACK))
         load_tab(1)
@@ -105,17 +108,17 @@ def tile_list_binding_setting_page_kernel(
         def load_states(t):
             nc.sync.dma_start(out=states[t][:], in_=page0_rows[t])
 
-        def load_wgs(t, first=0, count=S):
-            cols = slice(first, first + count)
+        def load_wgs(dst, first):
+            count = dst.shape[1]
             for q in range(4):
-                nc.sync.dma_start(out=wgs_sb[t][32 * q : 32 * (q + 1), cols], in_=wgs_rows[:, t, cols])
+                nc.sync.dma_start(out=dst[32 * q : 32 * (q + 1), :], in_=wgs_rows[:, first : first + count])
 
         def load_settings(c):
             nc.sync.dma_start(out=settings[c][:], in_=page1[c * P : (c + 1) * P, :])
 
-        picked = [kept(f"picked{a}", [P, S], U32) for a in range(PASSES)]
-        picked_plane = kept("picked_plane", [P, S], U8)
-        w1_codes = [kept(f"w1_codes{a}", [P, H], U32) for a in range(PASSES)]
+        picked = [placed(f"picked{a}", [P, S], U32, kib) for a, kib in enumerate((184, 176, 172))]
+        picked_plane = placed("picked_plane", [P, S], U8, 192)
+        w1_codes = [placed(f"w1_codes{a}", [P, H], U32, kib) for a, kib in enumerate((190, 92, 188))]
         w1_scales = [kept(f"w1_scales{a}", [P, H], U8) for a in range(PASSES)]
 
         def pick_words(a, first, count):
@@ -125,7 +128,7 @@ def tile_list_binding_setting_page_kernel(
             )
 
         def quantise_w1(a, engine_copy):
-            grouped = placed(f"w1_grouped{a}", [P, H, PACK], BF16, 160 + 4 * a)
+            grouped = placed(f"w1_grouped{a}", [P, H, PACK], BF16, (160, 180, 164)[a])
             engine_copy(
                 out=grouped[:].rearrange("p (t m) j -> p m t j", t=PACK),
                 in_=w1_raw[a][:].rearrange("p j (m t) -> p m t j", t=PACK),
@@ -164,19 +167,14 @@ def tile_list_binding_setting_page_kernel(
 
         nc.sync.dma_start(idx2[:], offs2)
         load_states(0)
-        load_wgs(0, 0, HALF)
-        load_wgs(0, HALF, HALF)
-        nc.sync.dma_start(out=w3_raw[:], in_=w3.rearrange("(p j) n -> p j n", j=PACK))
+        load_wgs(wgs_pair[:, :HALF], 0)
+        load_wgs(wgs_pair[:, HALF:], HALF)
         load_states(1)
-        load_wgs(1)
+        for i, (first, count) in enumerate(W3_PARTS):
+            nc.sync.dma_start(out=w3_raw[i][:], in_=w3.rearrange("(p j) n -> p j n", j=PACK)[:, :, first : first + count])
         with nc.allow_non_contiguous_dma(reason="one gain value a partition and output tile"):
             nc.sync.dma_start(out=gain_sb[:], in_=gain.rearrange("(c p) -> p c", p=P))
         load_states(2)
-        load_wgs(3)
-        load_settings(0)
-        load_settings(1)
-        load_settings(2)
-        load_states(3)
         nc.sync.dma_start(idx3[:], offs3)
         nc.sync.dma_start(idx4[:], offs4)
         nc.sync.dma_start(out=low_sb[:], in_=low.rearrange("(p t) -> p t", t=PACK))
@@ -186,10 +184,6 @@ def tile_list_binding_setting_page_kernel(
                 out=w2_plane[32 * q : 32 * q + 4, :].bitcast(I32),
                 in_=w2_scales[0, 4 * q : 4 * q + 4, :].bitcast(I32),
             )
-        nc.sync.dma_start(out=wgo_sb[:], in_=wgo)
-        load_settings(3)
-        load_settings(4)
-        load_settings(5)
 
         neg_gain = kept("neg_gain", [P, N_TILES], F32)
         nc.gpsimd.tensor_scalar(out=neg_gain[:], in0=gain_sb[:], scalar1=-1.0, scalar2=0.0, op0=ALU.mult, op1=ALU.add)
@@ -198,8 +192,9 @@ def tile_list_binding_setting_page_kernel(
 
         def cap_h(t, u):
             part = h[:, t, u * HALF : (u + 1) * HALF]
-            nc.scalar.copy(out=part, in_=h_banks[t, u][:])
-            nc.vector.tensor_scalar(out=part, in0=part, scalar1=cap_sb[:, t : t + 1], scalar2=None, op0=ALU.min)
+            sums = placed(f"sums{t}_{u}", [P, HALF], F32, (136, 138, 140, 142, 144, 88, 22, 24)[u * PACK + t])
+            nc.scalar.copy(out=sums[:], in_=h_banks[t, u][:])
+            nc.vector.tensor_scalar(out=part, in0=sums[:], scalar1=cap_sb[:, t : t + 1], scalar2=None, op0=ALU.min)
 
         def put_states(t, first, count):
             cols = slice(first, first + count)
@@ -219,7 +214,7 @@ def tile_list_binding_setting_page_kernel(
 
         def quantise_h(u):
             cols = slice(u * HALF, (u + 1) * HALF)
-            grouped = placed(f"h_grouped{u}", [P, HALF, PACK], BF16, 152 + 4 * u)
+            grouped = placed(f"h_grouped{u}", [P, HALF, PACK], BF16, (6, 38)[u])
             interleave(nc.scalar.copy, grouped[:], h[:, :, cols])
             quantise(h_codes[:, cols], h_scales[:, cols], grouped[:])
 
@@ -227,19 +222,23 @@ def tile_list_binding_setting_page_kernel(
         w3_scales = kept("w3_scales", [P, N], U8)
         put_states(1, 0, S)
         quantise_h(0)
-        w3_grouped = placed("w3_grouped", [P, N, PACK], BF16, 160)
-        interleave(nc.scalar.copy, w3_grouped[:], w3_raw[:])
-        load_wgs(2)
-        for first, count in ((0, 512), (512, 256)):
+        for i, (first, count) in enumerate(W3_PARTS):
             cols = slice(first, first + count)
-            quantise(w3_codes[:, cols], w3_scales[:, cols], w3_grouped[:, cols, :])
+            grouped = placed(f"w3_grouped{i}", [P, count, PACK], BF16, (22, 88)[i])
+            interleave(nc.scalar.copy, grouped[:], w3_raw[i][:])
+            load_wgs(wgs_sb[2 + i], (2 + i) * S)
+            quantise(w3_codes[:, cols], w3_scales[:, cols], grouped[:])
+        load_states(3)
+        nc.sync.dma_start(out=wgo_sb[:], in_=wgo)
         quantise_h(1)
         put_states(2, 0, S)
         put_states(3, 0, S)
+        for c in range(N_TILES):
+            load_settings(c)
 
         fresh = {}
 
-        def fresh_term(u, c):
+        def fresh_term(u, c, staged_at):
             cols = slice(u * HALF, (u + 1) * HALF)
             rows = slice(c * P, (c + 1) * P)
             e_bank = psum.tile([P, HALF], F32, name="bank")
@@ -252,7 +251,7 @@ def tile_list_binding_setting_page_kernel(
                 start=True,
                 stop=True,
             )
-            scaled = placed(f"scaled{u}_{c}", [P, HALF], F32, 150 + 2 * (c % 2))
+            scaled = placed(f"scaled{u}_{c}", [P, HALF], F32, staged_at + 2 * (c % 2))
             nc.scalar.activation(out=scaled[:], in_=e_bank[:], func=ACT.Copy, scale=neg_gain[:, c : c + 1])
             turned_bank = psum.tile([P, HALF], F32, name="bank")
             for b in range(HALF // P):
@@ -263,7 +262,7 @@ def tile_list_binding_setting_page_kernel(
 
         fresh_order = [(u, c) for u in range(HALVES) for c in range(N_TILES)]
         for u, c in fresh_order[:EARLY_GE]:
-            fresh_term(u, c)
+            fresh_term(u, c, 150)
 
         x_codes = kept("x_codes", [P, S], U32)
         x_scales = kept("x_scales", [P, S], U8)
@@ -326,7 +325,7 @@ def tile_list_binding_setting_page_kernel(
             settle(0, c)
         quantise_x(2)
         for u, c in fresh_order[EARLY_GE:]:
-            fresh_term(u, c)
+            fresh_term(u, c, 160)
         for s in range(1, len(X_SLICES)):
             for c in range(N_TILES):
                 settle(s, c)

@@ -64,13 +64,8 @@ def tile_list_binding_setting_page_kernel(
         idx3 = lists.tile([P, S // 16], U16, name="idx3")
         idx4 = lists.tile([P, S // 16], U16, name="idx4")
 
-        tab_plane = placed("tab_plane", [P, T], U8, 180)
-        nc.gpsimd.memset(tab_plane[:].bitcast(I32), 0)
-        for q in range(4):
-            nc.gpsimd.dma_start(
-                out=tab_plane[32 * q : 32 * q + 4 * PASSES, :].bitcast(I32),
-                in_=tab_scales[:, 4 * q : 4 * q + 4, :].bitcast(I32),
-            )
+        tab_plane = placed("tab_plane", [P, T], U8, 175)
+        nc.vector.memset(tab_plane[:].bitcast(I32), 0)
         w2_plane = kept("w2_plane", [P, N], U8)
         nc.vector.memset(w2_plane[:].bitcast(I32), 0)
         ident = kept("ident", [P, P], F32)
@@ -80,15 +75,17 @@ def tile_list_binding_setting_page_kernel(
         low_sb = kept("low_sb", [P, PACK], F32)
         gain_sb = kept("gain_sb", [P, N_TILES], F32)
         nc.scalar.dma_start(out=cap_sb[:], in_=cap.rearrange("(p t) -> p t", t=PACK))
+        with nc.allow_non_contiguous_dma(reason="one gain value a partition and output tile"):
+            nc.scalar.dma_start(out=gain_sb[:], in_=gain.rearrange("(c p) -> p c", p=P))
 
         tab = [placed(f"tab{a}", [P, T], I32, 16 * a) for a in range(PASSES)]
         w1_raw = [placed(f"w1_raw{a}", [P, PACK, H], F32, 48 + 8 * a) for a in range(PASSES)]
         states = [placed(f"states{t}", [P, T2], F32, kib) for t, kib in enumerate((72, 80, 184, 176))]
-        wgs_pair = placed("wgs_pair", [P, 2 * S], F32, 104)
-        wgs_late = [placed(f"wgs{t}", [P, S], F32, kib) for t, kib in ((2, 172), (3, 192))]
-        wgs_sb = [wgs_pair[:, :S], wgs_pair[:, S:], wgs_late[0][:], wgs_late[1][:]]
+        wgs_head = placed("wgs_head", [P, HALF], F32, 120)
+        wgs_next = placed("wgs_next", [P, HALF + S], F32, 192)
+        wgs_late = [placed(f"wgs{t}", [P, S], F32, kib) for t, kib in ((2, 172), (3, 42))]
         settings = [placed(f"settings{c}", [P, T2], F32, 8 * c) for c in range(N_TILES)]
-        w3_raw = [placed(f"w3_raw{i}", [P, PACK, count], F32, (172, 192)[i]) for i, (first, count) in enumerate(W3_PARTS)]
+        w3_raw = [placed(f"w3_raw{i}", [P, PACK, count], F32, (172, 40)[i]) for i, (first, count) in enumerate(W3_PARTS)]
         w2_codes = kept("w2_codes", [P, 2 * N], U8)
         wgo_sb = placed("wgo_sb", [P, S], F32, 88)
 
@@ -100,6 +97,11 @@ def tile_list_binding_setting_page_kernel(
 
         nc.sync.dma_start(idx[:], offs)
         load_tab(0)
+        for q in range(4):
+            nc.sync.dma_start(
+                out=tab_plane[32 * q : 32 * q + 4 * PASSES, :].bitcast(I32),
+                in_=tab_scales[:, 4 * q : 4 * q + 4, :].bitcast(I32),
+            )
         for a in range(PASSES):
             nc.sync.dma_start(out=w1_raw[a][:], in_=w1[512 * a : 512 * (a + 1), :].rearrange("(p j) r -> p j r", j=PACK))
         load_tab(1)
@@ -116,10 +118,10 @@ def tile_list_binding_setting_page_kernel(
         def load_settings(c):
             nc.sync.dma_start(out=settings[c][:], in_=page1[c * P : (c + 1) * P, :])
 
-        picked = [placed(f"picked{a}", [P, S], U32, kib) for a, kib in enumerate((184, 176, 172))]
-        picked_plane = placed("picked_plane", [P, S], U8, 192)
-        w1_codes = [placed(f"w1_codes{a}", [P, H], U32, kib) for a, kib in enumerate((190, 92, 188))]
-        w1_scales = [kept(f"w1_scales{a}", [P, H], U8) for a in range(PASSES)]
+        picked = [placed(f"picked{a}", [P, S], U32, kib) for a, kib in enumerate((184, 178, 172))]
+        picked_plane = kept("picked_plane", [P, S], U8)
+        w1_codes = [placed(f"w1_codes{a}", [P, H], U32, kib) for a, kib in enumerate((190, 92, 176))]
+        w1_scales = [placed(f"w1_scales{a}", [P, H], U8, kib) for a, kib in enumerate((94, 95, 188))]
 
         def pick_words(a, first, count):
             nc.vector.tensor_copy(
@@ -128,7 +130,7 @@ def tile_list_binding_setting_page_kernel(
             )
 
         def quantise_w1(a, engine_copy):
-            grouped = placed(f"w1_grouped{a}", [P, H, PACK], BF16, (160, 180, 164)[a])
+            grouped = placed(f"w1_grouped{a}", [P, H, PACK], BF16, 160 + 4 * a)
             engine_copy(
                 out=grouped[:].rearrange("p (t m) j -> p m t j", t=PACK),
                 in_=w1_raw[a][:].rearrange("p j (m t) -> p m t j", t=PACK),
@@ -167,13 +169,11 @@ def tile_list_binding_setting_page_kernel(
 
         nc.sync.dma_start(idx2[:], offs2)
         load_states(0)
-        load_wgs(wgs_pair[:, :HALF], 0)
-        load_wgs(wgs_pair[:, HALF:], HALF)
+        load_wgs(wgs_head[:], 0)
+        load_wgs(wgs_next[:], HALF)
         load_states(1)
         for i, (first, count) in enumerate(W3_PARTS):
             nc.sync.dma_start(out=w3_raw[i][:], in_=w3.rearrange("(p j) n -> p j n", j=PACK)[:, :, first : first + count])
-        with nc.allow_non_contiguous_dma(reason="one gain value a partition and output tile"):
-            nc.sync.dma_start(out=gain_sb[:], in_=gain.rearrange("(c p) -> p c", p=P))
         load_states(2)
         nc.sync.dma_start(idx3[:], offs3)
         nc.sync.dma_start(idx4[:], offs4)
@@ -186,54 +186,54 @@ def tile_list_binding_setting_page_kernel(
             )
 
         neg_gain = kept("neg_gain", [P, N_TILES], F32)
-        nc.gpsimd.tensor_scalar(out=neg_gain[:], in0=gain_sb[:], scalar1=-1.0, scalar2=0.0, op0=ALU.mult, op1=ALU.add)
+        nc.vector.tensor_scalar(out=neg_gain[:], in0=gain_sb[:], scalar1=-1.0, scalar2=0.0, op0=ALU.mult, op1=ALU.add)
 
         h = placed("h", [P, PACK, S], F32, 120)
 
         def cap_h(t, u):
-            part = h[:, t, u * HALF : (u + 1) * HALF]
             sums = placed(f"sums{t}_{u}", [P, HALF], F32, (136, 138, 140, 142, 144, 88, 22, 24)[u * PACK + t])
             nc.scalar.copy(out=sums[:], in_=h_banks[t, u][:])
+            part = sums[:] if (t, u) == (0, 0) else h[:, t, u * HALF : (u + 1) * HALF]
             nc.vector.tensor_scalar(out=part, in0=sums[:], scalar1=cap_sb[:, t : t + 1], scalar2=None, op0=ALU.min)
+            return part
 
-        def put_states(t, first, count):
-            cols = slice(first, first + count)
-            factors = wgs_sb[t][:, cols]
-            nc.vector.tensor_tensor(states[t][:].indirect(entries(idx2, first, count)), h[:, t, cols], factors, ALU.mult)
+        def put_states(t, first, values, factors):
+            nc.vector.tensor_tensor(states[t][:].indirect(entries(idx2, first, factors.shape[1])), values, factors, ALU.mult)
 
-        cap_h(0, 0)
-        put_states(0, 0, HALF)
+        h_head = cap_h(0, 0)
+        put_states(0, 0, h_head, wgs_head[:])
         for u in range(HALVES):
             for t in range(PACK):
                 if (t, u) != (0, 0):
                     cap_h(t, u)
-        put_states(0, HALF, HALF)
+        nc.scalar.copy(out=h[:, 0, :HALF], in_=h_head)
+        put_states(0, HALF, h[:, 0, HALF:], wgs_next[:, :HALF])
 
-        h_codes = kept("h_codes", [P, S], U32)
+        h_codes = [placed(f"h_codes{u}", [P, HALF], U32, kib) for u, kib in enumerate((192, 172))]
         h_scales = kept("h_scales", [P, S], U8)
 
         def quantise_h(u):
             cols = slice(u * HALF, (u + 1) * HALF)
             grouped = placed(f"h_grouped{u}", [P, HALF, PACK], BF16, (6, 38)[u])
             interleave(nc.scalar.copy, grouped[:], h[:, :, cols])
-            quantise(h_codes[:, cols], h_scales[:, cols], grouped[:])
+            quantise(h_codes[u][:], h_scales[:, cols], grouped[:])
 
-        w3_codes = kept("w3_codes", [P, N], U32)
+        w3_codes = [placed(f"w3_codes{i}", [P, count], U32, 194 + first * 4 // KIB) for i, (first, count) in enumerate(W3_PARTS)]
         w3_scales = kept("w3_scales", [P, N], U8)
-        put_states(1, 0, S)
+        put_states(1, 0, h[:, 1, :], wgs_next[:, HALF:])
         quantise_h(0)
         for i, (first, count) in enumerate(W3_PARTS):
             cols = slice(first, first + count)
             grouped = placed(f"w3_grouped{i}", [P, count, PACK], BF16, (22, 88)[i])
             interleave(nc.scalar.copy, grouped[:], w3_raw[i][:])
-            load_wgs(wgs_sb[2 + i], (2 + i) * S)
-            quantise(w3_codes[:, cols], w3_scales[:, cols], grouped[:])
+            load_wgs(wgs_late[i][:], (2 + i) * S)
+            quantise(w3_codes[i][:], w3_scales[:, cols], grouped[:])
         load_states(3)
         nc.sync.dma_start(out=wgo_sb[:], in_=wgo)
+        put_states(2, 0, h[:, 2, :], wgs_late[0][:])
         quantise_h(1)
-        put_states(2, 0, S)
-        put_states(3, 0, S)
-        for c in range(N_TILES):
+        put_states(3, 0, h[:, 3, :], wgs_late[1][:])
+        for c in range(N_TILES - 1):
             load_settings(c)
 
         fresh = {}
@@ -244,9 +244,9 @@ def tile_list_binding_setting_page_kernel(
             e_bank = psum.tile([P, HALF], F32, name="bank")
             nc.tensor.matmul_mx(
                 out=e_bank[:],
-                lhsT=w3_codes[:, rows].bitcast(FP8X4),
+                lhsT=w3_codes[c // 4][:, c % 4 * P : (c % 4 + 1) * P].bitcast(FP8X4),
                 lhsT_scale=w3_scales[:, rows],
-                rhs=h_codes[:, cols].bitcast(FP8X4),
+                rhs=h_codes[u][:].bitcast(FP8X4),
                 rhs_scale=h_scales[:, cols],
                 start=True,
                 stop=True,
@@ -266,7 +266,7 @@ def tile_list_binding_setting_page_kernel(
 
         x_codes = kept("x_codes", [P, S], U32)
         x_scales = kept("x_scales", [P, S], U8)
-        fetched_at = (136, 140, 144)
+        fetched_at = (136, 42, 144)
         grouped_at = (150, 152, 156)
         fetched = {}
 
@@ -320,6 +320,7 @@ def tile_list_binding_setting_page_kernel(
         recall(1)
         quantise_x(0)
         quantise_x(1)
+        load_settings(N_TILES - 1)
         recall(2)
         for c in range(N_TILES):
             settle(0, c)

@@ -24,9 +24,9 @@ HALF = 512
 HALVES = S // HALF
 N_TILES = N // P
 KIB = 1024
+BANK_BYTES = 2048
 X_SLICES = ((0, 256), (256, 256), (512, 512))
 W3_PARTS = ((0, 512), (512, 256))
-EARLY_GE = 9
 
 
 def tile_list_binding_setting_page_kernel(
@@ -37,12 +37,15 @@ def tile_list_binding_setting_page_kernel(
     with ExitStack() as ctx:
         lists = ctx.enter_context(tc.tile_pool(name="lists", bufs=1))
         keep = ctx.enter_context(tc.tile_pool(name="keep", bufs=1))
-        ring = ctx.enter_context(tc.tile_pool(name="ring", bufs=2))
+        ring = ctx.enter_context(tc.tile_pool(name="ring", bufs=3))
         laid = ctx.enter_context(tc.tile_pool(name="laid", bufs=1))
-        psum = ctx.enter_context(tc.psum_pool(name="psum", bufs=8))
+        psum = ctx.enter_context(tc.psum_pool(name="psum", bufs=1))
 
         def placed(name, shape, dtype, kib):
             return laid.tile(shape, dtype, name=name, offset=kib * KIB, align_bytes=64)
+
+        def bank(name, columns, number):
+            return psum.tile([P, columns], F32, name=name, offset=number * BANK_BYTES)
 
         def kept(name, shape, dtype):
             return keep.tile(shape, dtype, name=name, align_bytes=64)
@@ -64,8 +67,16 @@ def tile_list_binding_setting_page_kernel(
         idx3 = lists.tile([P, S // 16], U16, name="idx3")
         idx4 = lists.tile([P, S // 16], U16, name="idx4")
 
-        tab_plane = placed("tab_plane", [P, T], U8, 175)
-        nc.vector.memset(tab_plane[:].bitcast(I32), 0)
+        tab_plane = placed("tab_plane", [P, T], U8, 179)
+        nc.gpsimd.memset(tab_plane[:].bitcast(I32), 0)
+        for q in range(4):
+            nc.gpsimd.dma_start(
+                out=tab_plane[32 * q : 32 * q + 4 * PASSES, :].bitcast(I32),
+                in_=tab_scales[:, 4 * q : 4 * q + 4, :].bitcast(I32),
+            )
+        gain_rows = kept("gain_rows", [P, P], F32)
+        nc.vector.memset(gain_rows[:], 0.0)
+        nc.gpsimd.dma_start(out=gain_rows[:N_TILES, :], in_=gain.rearrange("(c p) -> c p", p=P))
         w2_plane = kept("w2_plane", [P, N], U8)
         nc.vector.memset(w2_plane[:].bitcast(I32), 0)
         ident = kept("ident", [P, P], F32)
@@ -73,10 +84,7 @@ def tile_list_binding_setting_page_kernel(
 
         cap_sb = kept("cap_sb", [P, PACK], F32)
         low_sb = kept("low_sb", [P, PACK], F32)
-        gain_sb = kept("gain_sb", [P, N_TILES], F32)
         nc.scalar.dma_start(out=cap_sb[:], in_=cap.rearrange("(p t) -> p t", t=PACK))
-        with nc.allow_non_contiguous_dma(reason="one gain value a partition and output tile"):
-            nc.scalar.dma_start(out=gain_sb[:], in_=gain.rearrange("(c p) -> p c", p=P))
 
         tab = [placed(f"tab{a}", [P, T], I32, 16 * a) for a in range(PASSES)]
         w1_raw = [placed(f"w1_raw{a}", [P, PACK, H], F32, 48 + 8 * a) for a in range(PASSES)]
@@ -97,12 +105,7 @@ def tile_list_binding_setting_page_kernel(
 
         nc.sync.dma_start(idx[:], offs)
         load_tab(0)
-        for q in range(4):
-            nc.sync.dma_start(
-                out=tab_plane[32 * q : 32 * q + 4 * PASSES, :].bitcast(I32),
-                in_=tab_scales[:, 4 * q : 4 * q + 4, :].bitcast(I32),
-            )
-        for a in range(PASSES):
+        for a in (2, 0, 1):
             nc.sync.dma_start(out=w1_raw[a][:], in_=w1[512 * a : 512 * (a + 1), :].rearrange("(p j) r -> p j r", j=PACK))
         load_tab(1)
         load_tab(2)
@@ -118,9 +121,9 @@ def tile_list_binding_setting_page_kernel(
         def load_settings(c):
             nc.sync.dma_start(out=settings[c][:], in_=page1[c * P : (c + 1) * P, :])
 
-        picked = [placed(f"picked{a}", [P, S], U32, kib) for a, kib in enumerate((184, 178, 172))]
+        picked = [placed(f"picked{a}", [P, S], U32, kib) for a, kib in enumerate((184, 56, 60))]
         picked_plane = kept("picked_plane", [P, S], U8)
-        w1_codes = [placed(f"w1_codes{a}", [P, H], U32, kib) for a, kib in enumerate((190, 92, 176))]
+        w1_codes = [placed(f"w1_codes{a}", [P, H], U32, kib) for a, kib in enumerate((190, 92, 178))]
         w1_scales = [placed(f"w1_scales{a}", [P, H], U8, kib) for a, kib in enumerate((94, 95, 188))]
 
         def pick_words(a, first, count):
@@ -129,13 +132,13 @@ def tile_list_binding_setting_page_kernel(
                 in_=tab[a][:].bitcast(U32).indirect(entries(idx, first, count)),
             )
 
-        def quantise_w1(a, engine_copy):
-            grouped = placed(f"w1_grouped{a}", [P, H, PACK], BF16, 160 + 4 * a)
+        def group_w1(a, engine_copy):
+            grouped = placed(f"w1_grouped{a}", [P, H, PACK], BF16, (160, 180, 164)[a])
             engine_copy(
                 out=grouped[:].rearrange("p (t m) j -> p m t j", t=PACK),
                 in_=w1_raw[a][:].rearrange("p j (m t) -> p m t j", t=PACK),
             )
-            quantise(w1_codes[a][:], w1_scales[a][:], grouped[:])
+            return grouped
 
         h_banks = {}
 
@@ -143,7 +146,7 @@ def tile_list_binding_setting_page_kernel(
             cols = slice(u * HALF, (u + 1) * HALF)
             for t in range(PACK):
                 if a == 0:
-                    h_banks[t, u] = psum.tile([P, HALF], F32, name="bank")
+                    h_banks[t, u] = bank(f"h_bank{t}_{u}", HALF, u * PACK + t)
                 rows = slice(t * P, (t + 1) * P)
                 nc.tensor.matmul_mx(
                     out=h_banks[t, u][:],
@@ -157,12 +160,14 @@ def tile_list_binding_setting_page_kernel(
 
         pick_words(0, 0, S)
         nc.vector.tensor_copy(out=picked_plane[:], in_=tab_plane[:].indirect(idx[:]))
-        quantise_w1(0, nc.scalar.copy)
-        quantise_w1(1, nc.vector.tensor_copy)
-        quantise_w1(2, nc.scalar.copy)
+        w1_last = group_w1(2, nc.scalar.copy)
+        for a in range(PASSES - 1):
+            quantise(w1_codes[a][:], w1_scales[a][:], group_w1(a, nc.vector.tensor_copy)[:])
         for u in range(HALVES):
             first_product(0, u)
         for a in range(1, PASSES):
+            if a == PASSES - 1:
+                quantise(w1_codes[a][:], w1_scales[a][:], w1_last[:])
             for u in range(HALVES):
                 pick_words(a, u * HALF, HALF)
                 first_product(a, u)
@@ -185,9 +190,6 @@ def tile_list_binding_setting_page_kernel(
                 in_=w2_scales[0, 4 * q : 4 * q + 4, :].bitcast(I32),
             )
 
-        neg_gain = kept("neg_gain", [P, N_TILES], F32)
-        nc.vector.tensor_scalar(out=neg_gain[:], in0=gain_sb[:], scalar1=-1.0, scalar2=0.0, op0=ALU.mult, op1=ALU.add)
-
         h = placed("h", [P, PACK, S], F32, 120)
 
         def cap_h(t, u):
@@ -207,6 +209,10 @@ def tile_list_binding_setting_page_kernel(
                 if (t, u) != (0, 0):
                     cap_h(t, u)
         nc.scalar.copy(out=h[:, 0, :HALF], in_=h_head)
+        gain_bank = bank("gain_bank", P, 0)
+        nc.tensor.transpose(gain_bank[:], gain_rows[:], ident[:])
+        neg_gain = kept("neg_gain", [P, N_TILES], F32)
+        nc.scalar.activation(out=neg_gain[:], in_=gain_bank[:, :N_TILES], func=ACT.Copy, scale=-1.0)
         put_states(0, HALF, h[:, 0, HALF:], wgs_next[:, :HALF])
 
         h_codes = [placed(f"h_codes{u}", [P, HALF], U32, kib) for u, kib in enumerate((192, 172))]
@@ -238,10 +244,10 @@ def tile_list_binding_setting_page_kernel(
 
         fresh = {}
 
-        def fresh_term(u, c, staged_at):
+        def fresh_term(u, c):
             cols = slice(u * HALF, (u + 1) * HALF)
             rows = slice(c * P, (c + 1) * P)
-            e_bank = psum.tile([P, HALF], F32, name="bank")
+            e_bank = bank(f"e_bank{u}_{c}", HALF, c)
             nc.tensor.matmul_mx(
                 out=e_bank[:],
                 lhsT=w3_codes[c // 4][:, c % 4 * P : (c % 4 + 1) * P].bitcast(FP8X4),
@@ -251,18 +257,12 @@ def tile_list_binding_setting_page_kernel(
                 start=True,
                 stop=True,
             )
-            scaled = placed(f"scaled{u}_{c}", [P, HALF], F32, staged_at + 2 * (c % 2))
-            nc.scalar.activation(out=scaled[:], in_=e_bank[:], func=ACT.Copy, scale=neg_gain[:, c : c + 1])
-            turned_bank = psum.tile([P, HALF], F32, name="bank")
-            for b in range(HALF // P):
-                block = slice(b * P, (b + 1) * P)
-                nc.tensor.transpose(turned_bank[:, block], scaled[:, block], ident[:])
             fresh[u, c] = placed(f"fresh{u}_{c}", [P, HALF], F32, 48 + 2 * (u * N_TILES + c))
-            nc.scalar.copy(out=fresh[u, c][:], in_=turned_bank[:])
+            nc.scalar.activation(out=fresh[u, c][:], in_=e_bank[:], func=ACT.Copy, scale=neg_gain[:, c : c + 1])
 
-        fresh_order = [(u, c) for u in range(HALVES) for c in range(N_TILES)]
-        for u, c in fresh_order[:EARLY_GE]:
-            fresh_term(u, c, 150)
+        for u in range(HALVES):
+            for c in range(N_TILES):
+                fresh_term(u, c)
 
         x_codes = kept("x_codes", [P, S], U32)
         x_scales = kept("x_scales", [P, S], U8)
@@ -286,35 +286,55 @@ def tile_list_binding_setting_page_kernel(
             interleave(nc.scalar.copy, grouped[:], fetched[s][:])
             quantise(x_codes[:, cols], x_scales[:, cols], grouped[:])
 
-        def settle(s, c):
+        units = [(s, c) for s in range(len(X_SLICES)) for c in range(N_TILES)]
+        gated = {}
+        turned = {}
+
+        def blocks_of(count):
+            return [slice(b * P, (b + 1) * P) for b in range(count // P)]
+
+        def gate(i):
+            s, c = units[i]
             first, count = X_SLICES[s]
-            blocks = count // P
-            b_bank = psum.tile([P, count], F32, name="bank")
-            for b in range(blocks):
-                cols = slice(first + b * P, first + (b + 1) * P)
-                nc.tensor.matmul_mx(
-                    out=b_bank[:, b * P : (b + 1) * P],
-                    lhsT=x_codes[:, cols].bitcast(FP8X4),
-                    lhsT_scale=x_scales[:, cols],
-                    rhs=w2_codes[:, 2 * c * P : 2 * (c + 1) * P].bitcast(FP4X4),
-                    rhs_scale=w2_plane[:, c * P : (c + 1) * P],
-                    start=True,
-                    stop=True,
-                )
-            gated = ring.tile([P, count], F32, name="gated")
-            nc.scalar.activation(out=gated[:], in_=b_bank[:], func=ACT.Silu)
-            y_bank = psum.tile([P, count], F32, name="bank")
+            cols = slice(first, first + count)
+            b_bank = bank(f"b_bank{i}", count, i % 2)
+            nc.tensor.matmul_mx(
+                out=b_bank[:],
+                lhsT=w2_codes[:, 2 * c * P : 2 * (c + 1) * P].bitcast(FP4X4),
+                lhsT_scale=w2_plane[:, c * P : (c + 1) * P],
+                rhs=x_codes[:, cols].bitcast(FP8X4),
+                rhs_scale=x_scales[:, cols],
+                start=True,
+                stop=True,
+            )
+            gated[i] = ring.tile([P, count], F32, name="gated")
+            nc.scalar.activation(out=gated[i][:], in_=b_bank[:], func=ACT.Silu)
+
+        def add_terms(i):
+            s, c = units[i]
+            first, count = X_SLICES[s]
             u, within = divmod(first, HALF)
-            for b in range(blocks):
-                block = slice(b * P, (b + 1) * P)
-                term = fresh[u, c][:, within + b * P : within + (b + 1) * P]
-                nc.tensor.matmul(y_bank[:, block], lhsT=term, rhs=ident[:], start=True, stop=False, is_transpose=True)
-                nc.tensor.matmul(y_bank[:, block], lhsT=gated[:, block], rhs=ident[:], start=False, stop=True, is_transpose=True)
-            y = placed(f"y{s}_{c}", [P, count], F32, 104 + (first * N_TILES + c * count) * 4 // KIB)
+            term = fresh[u, c][:, within : within + count]
+            sum_bank = bank(f"sum_bank{i}", count, 2 + i % 3)
+            for block in blocks_of(count):
+                nc.tensor.matmul(sum_bank[:, block], lhsT=term[:, block], rhs=ident[:], start=True, stop=False, is_transpose=True)
+                nc.tensor.matmul(sum_bank[:, block], lhsT=gated[i][:, block], rhs=ident[:], start=False, stop=True, is_transpose=True)
+            turned[i] = ring.tile([P, count], F32, name="turned")
+            nc.scalar.copy(out=turned[i][:], in_=sum_bank[:])
+
+        def put_settings(i):
+            s, c = units[i]
+            first, count = X_SLICES[s]
+            y_bank = bank(f"y_bank{i}", count, 5 + i % 3)
+            for block in blocks_of(count):
+                nc.tensor.transpose(y_bank[:, block], turned[i][:, block], ident[:])
+            y = placed(f"y{i}", [P, count], F32, 104 + (first * N_TILES + c * count) * 4 // KIB)
             nc.scalar.copy(out=y[:], in_=y_bank[:])
             nc.vector.tensor_tensor(
                 settings[c][:].indirect(entries(idx4, first, count)), y[:], wgo_sb[:, first : first + count], ALU.mult
             )
+            if first + count == S:
+                nc.sync.dma_start(out=out[c * P : (c + 1) * P, :], in_=settings[c][:])
 
         recall(0)
         recall(1)
@@ -322,13 +342,12 @@ def tile_list_binding_setting_page_kernel(
         quantise_x(1)
         load_settings(N_TILES - 1)
         recall(2)
-        for c in range(N_TILES):
-            settle(0, c)
-        quantise_x(2)
-        for u, c in fresh_order[EARLY_GE:]:
-            fresh_term(u, c, 160)
-        for s in range(1, len(X_SLICES)):
-            for c in range(N_TILES):
-                settle(s, c)
-                if s == len(X_SLICES) - 1:
-                    nc.sync.dma_start(out=out[c * P : (c + 1) * P, :], in_=settings[c][:])
+        for step in range(len(units) + 2):
+            if step == N_TILES + 2:
+                quantise_x(2)
+            if step < len(units):
+                gate(step)
+            if 1 <= step <= len(units):
+                add_terms(step - 1)
+            if step >= 2:
+                put_settings(step - 2)

from contextlib import ExitStack

import concourse.mybir as mybir
from concourse.masks import make_identity

K, T, S, H, T2, N = 1536, 4096, 1024, 512, 2048, 768
FLOPS = 2 * S * (K * H + 2 * H * N)

F32 = mybir.dt.float32
BF16 = mybir.dt.bfloat16
I32 = mybir.dt.int32
U32 = mybir.dt.uint32
U16 = mybir.dt.uint16
U8 = mybir.dt.uint8
FP8X4 = mybir.dt.float8_e4m3fn_x4
FP4X4 = mybir.dt.float4_e2m1fn_x4
ALU = mybir.AluOpType
ACT = mybir.ActivationFunctionType

P = 128
PACK = 4
PASSES = K // (P * PACK)
HALF = 512
HALVES = S // HALF
N_TILES = N // P
KIB = 1024
BANK_BYTES = 2048
X_SLICES = ((0, 256), (256, 256), (512, 512))
W3_PARTS = ((0, 512), (512, 256))


def tile_list_binding_setting_page_kernel(
    tc, tab_words, tab_scales, offs, w1, cap, page0, wgs, offs2, offs3, low, w2_words, w2_scales, w3, gain, page1, wgo, offs4, out
):
    nc = tc.nc

    with ExitStack() as ctx:
        lists = ctx.enter_context(tc.tile_pool(name="lists", bufs=1))
        keep = ctx.enter_context(tc.tile_pool(name="keep", bufs=1))
        ring = ctx.enter_context(tc.tile_pool(name="ring", bufs=3))
        laid = ctx.enter_context(tc.tile_pool(name="laid", bufs=1))
        psum = ctx.enter_context(tc.psum_pool(name="psum", bufs=1))

        def placed(name, shape, dtype, kib):
            return laid.tile(shape, dtype, name=name, offset=kib * KIB, align_bytes=64)

        def bank(name, columns, number):
            return psum.tile([P, columns], F32, name=name, offset=number * BANK_BYTES)

        def kept(name, shape, dtype):
            return keep.tile(shape, dtype, name=name, align_bytes=64)

        def entries(offsets, first, count):
            return offsets[:, first // 16 : (first + count) // 16]

        def interleave(engine_copy, dst, src):
            engine_copy(
                out=dst.rearrange("p (c i) t -> p c t i", i=PACK),
                in_=src.rearrange("p t (c i) -> p c t i", i=PACK),
            )

        def quantise(codes, scales, grouped):
            nc.vector.quantize_mx(out=codes.bitcast(FP8X4), scales=scales, in_=grouped.rearrange("p c t -> p (c t)"))

        idx = lists.tile([P, S // 16], U16, name="idx")
        idx2 = lists.tile([P, S // 16], U16, name="idx2")
        idx3 = lists.tile([P, S // 16], U16, name="idx3")
        idx4 = lists.tile([P, S // 16], U16, name="idx4")

        tab_plane = placed("tab_plane", [P, T], U8, 179)
        nc.gpsimd.memset(tab_plane[:].bitcast(I32), 0)
        for q in range(4):
            nc.gpsimd.dma_start(
                out=tab_plane[32 * q : 32 * q + 4 * PASSES, :].bitcast(I32),
                in_=tab_scales[:, 4 * q : 4 * q + 4, :].bitcast(I32),
            )
        gain_rows = kept("gain_rows", [P, P], F32)
        nc.vector.memset(gain_rows[:], 0.0)
        nc.gpsimd.dma_start(out=gain_rows[:N_TILES, :], in_=gain.rearrange("(c p) -> c p", p=P))
        w2_plane = kept("w2_plane", [P, N], U8)
        nc.vector.memset(w2_plane[:].bitcast(I32), 0)
        ident = kept("ident", [P, P], F32)
        make_identity(nc, ident[:])

        cap_sb = kept("cap_sb", [P, PACK], F32)
        low_sb = kept("low_sb", [P, PACK], F32)
        nc.scalar.dma_start(out=cap_sb[:], in_=cap.rearrange("(p t) -> p t", t=PACK))

        tab = [placed(f"tab{a}", [P, T], I32, 16 * a) for a in range(PASSES)]
        w1_raw = [placed(f"w1_raw{a}", [P, PACK, H], F32, 48 + 8 * a) for a in range(PASSES)]
        states = [placed(f"states{t}", [P, T2], F32, kib) for t, kib in enumerate((72, 80, 184, 176))]
        wgs_head = placed("wgs_head", [P, HALF], F32, 120)
        wgs_next = placed("wgs_next", [P, HALF + S], F32, 192)
        wgs_late = [placed(f"wgs{t}", [P, S], F32, kib) for t, kib in ((2, 172), (3, 42))]
        settings = [placed(f"settings{c}", [P, T2], F32, 8 * c) for c in range(N_TILES)]
        w3_raw = [placed(f"w3_raw{i}", [P, PACK, count], F32, (172, 40)[i]) for i, (first, count) in enumerate(W3_PARTS)]
        w2_codes = kept("w2_codes", [P, 2 * N], U8)
        wgo_sb = placed("wgo_sb", [P, S], F32, 88)

        def load_tab(a):
            nc.sync.dma_start(out=tab[a][:], in_=tab_words[a].rearrange("p t i -> p (t i)").bitcast(I32))

        page0_rows = page0.rearrange("(p t) c -> t p c", t=PACK)
        wgs_rows = wgs.rearrange("(q t) s -> q (t s)", t=PACK)

        nc.sync.dma_start(idx[:], offs)
        load_tab(0)
        for a in (2, 0, 1):
            nc.sync.dma_start(out=w1_raw[a][:], in_=w1[512 * a : 512 * (a + 1), :].rearrange("(p j) r -> p j r", j=PACK))
        load_tab(1)
        load_tab(2)

        def load_states(t):
            nc.sync.dma_start(out=states[t][:], in_=page0_rows[t])

        def load_wgs(dst, first):
            count = dst.shape[1]
            for q in range(4):
                nc.sync.dma_start(out=dst[32 * q : 32 * (q + 1), :], in_=wgs_rows[:, first : first + count])

        def load_settings(c):
            nc.sync.dma_start(out=settings[c][:], in_=page1[c * P : (c + 1) * P, :])

        picked = [placed(f"picked{a}", [P, S], U32, kib) for a, kib in enumerate((184, 56, 60))]
        picked_plane = kept("picked_plane", [P, S], U8)
        w1_codes = [placed(f"w1_codes{a}", [P, H], U32, kib) for a, kib in enumerate((190, 92, 178))]
        w1_scales = [placed(f"w1_scales{a}", [P, H], U8, kib) for a, kib in enumerate((94, 95, 188))]

        def pick_words(a, first, count):
            nc.vector.tensor_copy(
                out=picked[a][:, first : first + count],
                in_=tab[a][:].bitcast(U32).indirect(entries(idx, first, count)),
            )

        def group_w1(a, engine_copy):
            grouped = placed(f"w1_grouped{a}", [P, H, PACK], BF16, (160, 180, 164)[a])
            engine_copy(
                out=grouped[:].rearrange("p (t m) j -> p m t j", t=PACK),
                in_=w1_raw[a][:].rearrange("p j (m t) -> p m t j", t=PACK),
            )
            return grouped

        h_banks = {}

        def first_product(a, u):
            cols = slice(u * HALF, (u + 1) * HALF)
            for t in range(PACK):
                if a == 0:
                    h_banks[t, u] = bank(f"h_bank{t}_{u}", HALF, u * PACK + t)
                rows = slice(t * P, (t + 1) * P)
                nc.tensor.matmul_mx(
                    out=h_banks[t, u][:],
                    lhsT=w1_codes[a][:, rows].bitcast(FP8X4),
                    lhsT_scale=w1_scales[a][:, rows],
                    rhs=picked[a][:, cols].bitcast(FP8X4),
                    rhs_scale=picked_plane[4 * a :, cols],
                    start=(a == 0),
                    stop=(a == PASSES - 1),
                )

        pick_words(0, 0, S)
        nc.vector.tensor_copy(out=picked_plane[:], in_=tab_plane[:].indirect(idx[:]))
        w1_last = group_w1(2, nc.scalar.copy)
        for a in range(PASSES - 1):
            quantise(w1_codes[a][:], w1_scales[a][:], group_w1(a, nc.vector.tensor_copy)[:])
        for u in range(HALVES):
            first_product(0, u)
        for a in range(1, PASSES):
            if a == PASSES - 1:
                quantise(w1_codes[a][:], w1_scales[a][:], w1_last[:])
            for u in range(HALVES):
                pick_words(a, u * HALF, HALF)
                first_product(a, u)

        nc.sync.dma_start(idx2[:], offs2)
        load_states(0)
        load_wgs(wgs_head[:], 0)
        load_wgs(wgs_next[:], HALF)
        load_states(1)
        for i, (first, count) in enumerate(W3_PARTS):
            nc.sync.dma_start(out=w3_raw[i][:], in_=w3.rearrange("(p j) n -> p j n", j=PACK)[:, :, first : first + count])
        load_states(2)
        nc.sync.dma_start(idx3[:], offs3)
        nc.sync.dma_start(idx4[:], offs4)
        nc.sync.dma_start(out=low_sb[:], in_=low.rearrange("(p t) -> p t", t=PACK))
        nc.sync.dma_start(out=w2_codes[:].bitcast(I32), in_=w2_words[0].bitcast(I32))
        for q in range(4):
            nc.sync.dma_start(
                out=w2_plane[32 * q : 32 * q + 4, :].bitcast(I32),
                in_=w2_scales[0, 4 * q : 4 * q + 4, :].bitcast(I32),
            )

        h = placed("h", [P, PACK, S], F32, 120)

        def cap_h(t, u):
            sums = placed(f"sums{t}_{u}", [P, HALF], F32, (136, 138, 140, 142, 144, 88, 22, 24)[u * PACK + t])
            nc.scalar.copy(out=sums[:], in_=h_banks[t, u][:])
            part = sums[:] if (t, u) == (0, 0) else h[:, t, u * HALF : (u + 1) * HALF]
            nc.vector.tensor_scalar(out=part, in0=sums[:], scalar1=cap_sb[:, t : t + 1], scalar2=None, op0=ALU.min)
            return part

        def put_states(t, first, values, factors):
            nc.vector.tensor_tensor(states[t][:].indirect(entries(idx2, first, factors.shape[1])), values, factors, ALU.mult)

        h_head = cap_h(0, 0)
        put_states(0, 0, h_head, wgs_head[:])
        for u in range(HALVES):
            for t in range(PACK):
                if (t, u) != (0, 0):
                    cap_h(t, u)
        nc.scalar.copy(out=h[:, 0, :HALF], in_=h_head)
        gain_bank = bank("gain_bank", P, 0)
        nc.tensor.transpose(gain_bank[:], gain_rows[:], ident[:])
        neg_gain = kept("neg_gain", [P, N_TILES], F32)
        nc.scalar.activation(out=neg_gain[:], in_=gain_bank[:, :N_TILES], func=ACT.Copy, scale=-1.0)
        put_states(0, HALF, h[:, 0, HALF:], wgs_next[:, :HALF])

        h_codes = [placed(f"h_codes{u}", [P, HALF], U32, kib) for u, kib in enumerate((192, 172))]
        h_scales = kept("h_scales", [P, S], U8)

        def quantise_h(u):
            cols = slice(u * HALF, (u + 1) * HALF)
            grouped = placed(f"h_grouped{u}", [P, HALF, PACK], BF16, (6, 38)[u])
            interleave(nc.scalar.copy, grouped[:], h[:, :, cols])
            quantise(h_codes[u][:], h_scales[:, cols], grouped[:])

        w3_codes = [placed(f"w3_codes{i}", [P, count], U32, 194 + first * 4 // KIB) for i, (first, count) in enumerate(W3_PARTS)]
        w3_scales = kept("w3_scales", [P, N], U8)
        put_states(1, 0, h[:, 1, :], wgs_next[:, HALF:])
        quantise_h(0)
        for i, (first, count) in enumerate(W3_PARTS):
            cols = slice(first, first + count)
            grouped = placed(f"w3_grouped{i}", [P, count, PACK], BF16, (22, 88)[i])
            interleave(nc.scalar.copy, grouped[:], w3_raw[i][:])
            load_wgs(wgs_late[i][:], (2 + i) * S)
            quantise(w3_codes[i][:], w3_scales[:, cols], grouped[:])
        load_states(3)
        nc.sync.dma_start(out=wgo_sb[:], in_=wgo)
        put_states(2, 0, h[:, 2, :], wgs_late[0][:])
        quantise_h(1)
        put_states(3, 0, h[:, 3, :], wgs_late[1][:])
        for c in range(N_TILES - 1):
            load_settings(c)

        fresh = {}

        def fresh_term(u, c):
            cols = slice(u * HALF, (u + 1) * HALF)
            rows = slice(c * P, (c + 1) * P)
            e_bank = bank(f"e_bank{u}_{c}", HALF, c)
            nc.tensor.matmul_mx(
                out=e_bank[:],
                lhsT=w3_codes[c // 4][:, c % 4 * P : (c % 4 + 1) * P].bitcast(FP8X4),
                lhsT_scale=w3_scales[:, rows],
                rhs=h_codes[u][:].bitcast(FP8X4),
                rhs_scale=h_scales[:, cols],
                start=True,
                stop=True,
            )
            fresh[u, c] = placed(f"fresh{u}_{c}", [P, HALF], F32, 48 + 2 * (u * N_TILES + c))
            nc.scalar.activation(out=fresh[u, c][:], in_=e_bank[:], func=ACT.Copy, scale=neg_gain[:, c : c + 1])

        for u in range(HALVES):
            for c in range(N_TILES):
                fresh_term(u, c)

        x_codes = kept("x_codes", [P, S], U32)
        x_scales = kept("x_scales", [P, S], U8)
        fetched_at = (136, 42, 144)
        grouped_at = (150, 152, 156)
        fetched = {}

        def recall(s):
            first, count = X_SLICES[s]
            x = placed(f"x{s}", [P, PACK, count], F32, fetched_at[s])
            for t in range(PACK):
                nc.vector.tensor_copy(out=x[:, t, :], in_=states[t][:].indirect(entries(idx3, first, count)))
            for t in range(PACK):
                nc.vector.tensor_scalar(out=x[:, t, :], in0=x[:, t, :], scalar1=low_sb[:, t : t + 1], scalar2=None, op0=ALU.max)
            fetched[s] = x

        def quantise_x(s):
            first, count = X_SLICES[s]
            cols = slice(first, first + count)
            grouped = placed(f"x_grouped{s}", [P, count, PACK], BF16, grouped_at[s])
            interleave(nc.scalar.copy, grouped[:], fetched[s][:])
            quantise(x_codes[:, cols], x_scales[:, cols], grouped[:])

        units = [(s, c) for s in range(len(X_SLICES)) for c in range(N_TILES)]
        gated = {}
        turned = {}

        def blocks_of(count):
            return [slice(b * P, (b + 1) * P) for b in range(count // P)]

        def gate(i):
            s, c = units[i]
            first, count = X_SLICES[s]
            cols = slice(first, first + count)
            b_bank = bank(f"b_bank{i}", count, i % 2)
            nc.tensor.matmul_mx(
                out=b_bank[:],
                lhsT=w2_codes[:, 2 * c * P : 2 * (c + 1) * P].bitcast(FP4X4),
                lhsT_scale=w2_plane[:, c * P : (c + 1) * P],
                rhs=x_codes[:, cols].bitcast(FP8X4),
                rhs_scale=x_scales[:, cols],
                start=True,
                stop=True,
            )
            gated[i] = ring.tile([P, count], F32, name="gated")
            nc.scalar.activation(out=gated[i][:], in_=b_bank[:], func=ACT.Silu)

        def add_terms(i):
            s, c = units[i]
            first, count = X_SLICES[s]
            u, within = divmod(first, HALF)
            term = fresh[u, c][:, within : within + count]
            sum_bank = bank(f"sum_bank{i}", count, 2 + i % 3)
            for block in blocks_of(count):
                nc.tensor.matmul(sum_bank[:, block], lhsT=term[:, block], rhs=ident[:], start=True, stop=False, is_transpose=True)
                nc.tensor.matmul(sum_bank[:, block], lhsT=gated[i][:, block], rhs=ident[:], start=False, stop=True, is_transpose=True)
            turned[i] = ring.tile([P, count], F32, name="turned")
            nc.scalar.copy(out=turned[i][:], in_=sum_bank[:])

        def put_settings(i):
            s, c = units[i]
            first, count = X_SLICES[s]
            y_bank = bank(f"y_bank{i}", count, 5 + i % 3)
            for block in blocks_of(count):
                nc.tensor.transpose(y_bank[:, block], turned[i][:, block], ident[:])
            y = placed(f"y{i}", [P, count], F32, 104 + (first * N_TILES + c * count) * 4 // KIB)
            nc.scalar.copy(out=y[:], in_=y_bank[:])
            nc.vector.tensor_tensor(
                settings[c][:].indirect(entries(idx4, first, count)), y[:], wgo_sb[:, first : first + count], ALU.mult
            )
            if first + count == S:
                nc.sync.dma_start(out=out[c * P : (c + 1) * P, :], in_=settings[c][:])

        recall(0)
        recall(1)
        quantise_x(0)
        quantise_x(1)
        load_settings(N_TILES - 1)
        recall(2)
        for step in range(len(units) + 2):
            if step == N_TILES + 2:
                quantise_x(2)
            if step < len(units):
                gate(step)
            if 1 <= step <= len(units):
                add_terms(step - 1)
            if step >= 2:
                put_settings(step - 2)
